import numpy as np, ml_dtypes
CORES = [16,17,18,19,32,33,34,35]
N = 8
import mx_ref
BF = ml_dtypes.bfloat16
def tile(rs):
    return np.stack(rs, axis=2).reshape(128, -1).astype(BF)
def pick(q, e):
    c = np.concatenate([q[0].reshape(128, -1, 4), np.zeros((128, 1, 4), np.uint8)], axis=1); s = np.concatenate([q[1], np.ones((16, 1), np.uint8)], axis=1)
    return (np.ascontiguousarray(c[:, e].reshape(128, -1)), np.ascontiguousarray(s[:, e]))
def join(*qs):
    return (np.concatenate([q[0] for q in qs], axis=1), np.concatenate([q[1] for q in qs], axis=1))
def put(q, e, v):
    c, s = q[0].reshape(128, -1, 4).copy(), q[1].copy(); c[:, e] = v[0].reshape(128, -1, 4); s[:, e] = v[1]
    return (c.reshape(128, -1), s)
def pk(c, s):
    return (np.ascontiguousarray(c), mx_ref.live(s))
def emit(q):
    return q[0], q[1]
def packed(v, rng):
    q = [mx_ref.quantize(np.ascontiguousarray(v[r])) for r in range(N)]
    return np.stack([a for a, b in q]), np.stack([mx_ref.plane(b, rng) for a, b in q])
def values_of_codes():
    e, c = np.zeros((128, 128, 4), np.float32), np.zeros((128, 2, 4), np.uint8)
    e[np.arange(128), np.arange(128), 0] = 1
    c[:127, :, 0] = np.arange(256).reshape(2, 128).T[:127]
    return mx_ref.matmul(mx_ref.quantize(e.reshape(128, 512).astype(BF)), (c.reshape(128, 8), np.full((16, 2), 127, np.uint8))).T.reshape(-1).astype(np.float64)
CODE_VALUE, SCALE_VALUE = values_of_codes(), 2.0 ** (np.arange(256) - 127.0)
def decode(q):
    return (CODE_VALUE[q[0]].reshape(16, 8, -1, 4) * SCALE_VALUE[q[1]][:, None, :, None] + 0.0).reshape(128, -1).astype(np.float32)
def f(rng, *shape):
    return mx_ref.flush((rng.standard_normal(shape, dtype=np.float32) * np.exp2(rng.integers(-2, 3, shape[:-1] + (1,)))).astype(BF))
def wide(rng, *shape, cols=0):
    v = rng.standard_normal(shape, dtype=np.float32) * np.exp2(rng.integers(-12, 13, shape)).astype(np.float32)
    if cols: v *= np.repeat(np.exp2(rng.integers(-cols, cols + 1, shape[:-2] + (1, shape[-1] // 4))) * (rng.random(shape[:-2] + (1, shape[-1] // 4)) > 0.0625), 4, axis=-1).astype(np.float32)
    return mx_ref.flush(v.astype(BF))
C, E, K = 320, 4, 80
STEP = [1, 2, 4]
def numbers_of(rng):
    return {"x": np.array(f(rng, N, 128, 4 * C)), "u": np.array(f(rng, N, 128, 512)), "v": np.array(f(rng, N, 128, 512))}
def layers(rng):
    return np.array(f(rng, N, 128, 2048)).reshape(N, 8, 16, 4, 8, 16, 4)
def held(w, parts):
    for i in parts:
        w[:, :, i] = 0
        w[:, :, :, :, :, i] = 0
    for i in parts:
        for g in range(8):
            for b in range(4): w[:, g, i, b, g, i, b] = 64
    return w
def weights(rng, w):
    c, p = packed(np.ascontiguousarray(w).reshape(N, 128, 2048), rng)
    return {"wc": c, "ws": p}
def setup_inputs(rng):
    return {**numbers_of(rng), **weights(rng, layers(rng))}
def setup_inputs_ties(rng):
    d = numbers_of(rng)
    x = d["x"].astype(np.float32).reshape(N, 8, 16, C, 4)
    x[:, :, 0] = 0
    x[:, :, 0, :, 0] = rng.integers(0, 4, (N, 8, C))
    z = (N, 8, 8, C, 4)
    x[:, :, 8:] = (2 * rng.integers(0, 8, z) + 1) * (2.0 * rng.integers(0, 2, z) - 1.0) * np.exp2(-1.0 * rng.integers(12, 19, z))
    x[:, :, 8, :, 0] = 1.96875
    u = d["u"].reshape(N, 128, 128, 4)
    u[:, :, ::16] = 0
    o = rng.permutation(N)
    for r in range(N):
        for h in range(0, 128, 16): u[r, h, h, 0] = 0.0 if r == o[0] else -1.0 if r == o[1] else 1.0
    w = layers(rng)
    w[:, :, 8, :, :, :, 0] = 0
    for r in o[3::2]:
        k = (r + STEP[0]) % N
        w[k, :, :, :, :, 8:] = 0
        for g in range(8):
            x[r, g, 8, :, 0] = 1.125
            x[r, g, 9, :, 0] = (3 + 2 * (g % 2)) * 2.0 ** (-14 - g // 2)
            u[r, 16 * g + 9, 16 * g, 0] = 1.0
            w[k, g, 8, 0, g, 8, 0] = 56
            w[k, g, 9, 0, g, 9, 0] = 32
    return {"x": x.reshape(N, 128, 4 * C).astype(BF), "u": u.reshape(N, 128, 512), "v": d["v"], **weights(rng, held(w, [0]))}
def setup_inputs_near(rng):
    d = numbers_of(rng)
    x = d["x"].astype(np.float32).reshape(N, 8, 16, C, 4)
    x[:, :, 0] = 0
    x[:, :, 8:] = 0
    x[:, :, 0, :, 0] = rng.integers(0, 2, (N, 8, C)) * 2.0 - 1.0
    s = rng.integers(0, 16, (N, 8, C))
    x[:, :, 8] = ((s[:, :, :, None] >> np.arange(4)) & 1) * np.exp2(np.arange(4) - 23.0)
    x[:, :, 11, :, 0] = 2.0 ** -10
    u = d["u"].reshape(N, 128, 128, 4)
    u[:, :, ::16] = 0
    o = rng.permutation(N) % 4
    for r in range(N):
        k = 1.0 if o[r] == 0 else 2.0 ** -30
        if o[r] == 2:
            x[r, :, 0] = 0
            x[r, :, 11] = 0
            for g in rng.permutation(8)[:4]: x[r, g, 0, rng.integers(C), 0] = 2.0 ** 16 * rng.choice([-1.0, 1.0])
        if o[r] == 3:
            x[r, :, 0] = 0
            x[r, :, 8:] = 0
            x[r, :, 10, :, 0] = rng.integers(-4, 5, (8, C)) * 2.0 ** -30
        for h in range(0, 128, 16):
            if o[r] < 2:
                u[r, h, h, 0] = k
                u[r, h + 11, h, 0] = k
            if o[r] == 2: u[r, h, h, 0] = 1.0
            if o[r] < 3: u[r, h + 8, h] = k
            else: u[r, h + 10, h, 0] = k
    w = held(layers(rng), [0, 8, 9, 10, 11, 12, 13, 14, 15])
    return {"x": x.reshape(N, 128, 4 * C).astype(BF), "u": u.reshape(N, 128, 512), "v": d["v"], **weights(rng, w)}
def setup_inputs_huge(rng):
    d = numbers_of(rng)
    o = rng.permutation(N)
    x = (0.8 + 0.2 * rng.random((N, 8, 16, C, 4))) * 1.4 * 2.0 ** 25
    c = rng.integers(0, 2, (N, 1, 1, C, 1)) * 2.0 - 1.0
    c[o < N // 2] = -1.0
    u = d["u"].reshape(N, 128, 128, 4)
    for r in range(N):
        a = 2.0 ** 30 * (1.0 - 0.1 * rng.random((128, 8, 4))) * (rng.permutation(8) % 2 * 2.0 - 1.0)[None, :, None]
        u[r, :, ::16] = a.astype(np.float32).astype(BF)
    w = np.zeros((N, 128, 4, 128, 4), np.float32)
    i = np.arange(128)
    for b in range(4): w[:, i, b, i, b] = 8
    return {"x": (x * c).astype(np.float32).reshape(N, 128, 4 * C).astype(BF), "u": u.reshape(N, 128, 512), "v": d["v"], **weights(rng, w.astype(BF))}
def setup_inputs_ends(rng):
    d = numbers_of(rng)
    e = rng.permutation(N)
    a = np.float32(1.9375 * 2.0 ** 25)
    x = d["x"].astype(np.float32).reshape(N, 8, 16, C, 4)
    u = d["u"].reshape(N, 128, 128, 4)
    u[:, :, ::16] = (2.0 ** 30 * rng.choice([-1.0, 1.0], (N, 1, 8, 1))).astype(np.float32).astype(BF)
    for r in range(N):
        if r == e[0]: x[r] = -a
        elif r == e[1]: x[r] = a * rng.choice([-1.0, 1.0], (1, 1, C, 1))
        elif r == e[2]: x[r] = a * rng.choice([-1.0, 1.0], (8, 16, C, 4))
        elif r == e[3]:
            x[r, :, 8:] = 0
            x[r, :, 8, :, 0] = rng.integers(-1, 2, (8, C)) * 2.0 ** -30
            u[r, :, ::16] = 0
            for h in range(0, 128, 16): u[r, h + 8, h, 0] = 2.0 ** -30
        else: x[r] = -a * rng.choice([0.5, 1.0], (8, 16, C, 4))
    w = layers(rng).astype(np.float32) * np.float32(2.0 ** -10)
    w[:, :, :, :, :, 8:] = 0
    d["v"] = (np.where(d["v"] < 0, -1.0, 1.0) * np.where(rng.permutation(N) % 2, 2.0 ** -30, 2.0 ** 30)[:, None, None]).astype(np.float32).astype(BF)
    return {"x": x.reshape(N, 128, 4 * C).astype(BF), "u": u.reshape(N, 128, 512), "v": d["v"], **weights(rng, mx_ref.flush(w.astype(BF)))}
def setup_inputs_spread(rng):
    d = setup_inputs(rng)
    d["x"] = np.clip(wide(rng, N, 128, 4 * C, cols=3).astype(np.float32), -65536.0, 65536.0).astype(BF)
    return d
def check_inputs(d):
    b = []
    for k in ("x", "u", "v"):
        a = np.abs(d[k].astype(np.float32))
        if not (np.isfinite(a).all() and ((a == 0) | (a >= 2.0 ** -30) & (a <= 2.0 ** 30)).all()): b.append("a value of " + k)
    none, least, most = [emit(mx_ref.quantize(np.full((128, 16), k, np.float32).astype(BF)))[1][0, 0] for k in (0.0, 2.0 ** -30, 2.0 ** 30)]
    top = 0.0
    for r in range(N):
        if ((d["wc"][r] == 0x7F) | (d["wc"][r] == 0xFF)).any(): b.append("wc: a code that is no number")
        s = mx_ref.live(d["ws"][r])
        if ((s != none) & ((s < least) | (s > most))).any(): b.append("ws: a scale out of range")
        w = np.abs(decode(pk(d["wc"][r], d["ws"][r])).astype(np.float64)).reshape(128, 512, 4)
        top = max(top, float(np.max(np.sum(w, axis=(0, 2)))))
    g = min(2.5 + 0.02 * top, 1e60)
    if not g * g * g * float(np.max(np.abs(d["x"].astype(np.float32)))) <= 2.0 ** 30: b.append("x and W: the bound of what they make")
    return b
def reference(x, u, v, wc, ws):
    qu = [mx_ref.quantize(u[r]) for r in range(N)]
    lay = [[pick(pk(wc[r], ws[r]), np.arange(128 * b, 128 * b + 128)) for b in range(4)] for r in range(N)]
    now = [x[r] for r in range(N)]
    for t in range(len(STEP)):
        first = np.arange(t % 2, 8, 2)
        second = (first + 1) % 8
        made = []
        for r in range(N):
            q = mx_ref.quantize(now[r])
            s = mx_ref.matmul(qu[r], q)[::16] + np.float32(0.0)
            o = np.argsort(-s, axis=1, kind="stable")[:, None, :, None]
            a = np.take_along_axis(decode(q).reshape(8, 16, C, 4), o, axis=2).reshape(8, 16, K, E, 4)
            m = np.max(a, axis=3)
            qm = mx_ref.quantize(np.ascontiguousarray(m.reshape(128, 4 * K)).astype(BF))
            back = mx_ref.quantize(tile([mx_ref.matmul(w, qm) * np.float32(0.015625) for w in lay[(r + STEP[t]) % N]]))
            p = decode(back).reshape(8, 16, K, 4)
            c = mx_ref.matmul(qu[r], back)[::16] + np.float32(0.0)
            swap = c[first] < c[second]
            source = np.zeros((8, K), np.int64)
            source[first] = np.where(swap, second[:, None], first[:, None])
            source[second] = np.where(swap, first[:, None], second[:, None])
            away = (a - m[:, :, :, None]).transpose(0, 2, 1, 3, 4)[source, np.arange(K)].transpose(0, 2, 1, 3, 4)
            new = np.zeros((8, 16, C, 4), np.float32)
            np.put_along_axis(new, o, (away + p[:, :, :, None]).reshape(8, 16, C, 4), axis=2)
            made.append(new.reshape(128, 4 * C).astype(BF))
        now = made
    y = np.zeros((N, 128, C), np.float32)
    oc, osc = np.zeros((N, 128, 4 * C), np.uint8), np.zeros((N, 16, C), np.uint8)
    for r in range(N):
        q = mx_ref.quantize(now[r])
        y[r] = mx_ref.matmul(mx_ref.quantize(v[r]), q)
        oc[r], osc[r] = emit(q)
    return {"y": y, "oc": oc, "osc": osc}

from concourse.mybir import dt, AluOpType, ActivationFunctionType

ALU = AluOpType
ACT = ActivationFunctionType
BF, F32, I32, U16, U8, MX = "bfloat16", "float32", "int32", "uint16", "uint8", "float8_e4m3fn_x4"
C, K, STEP = 320, 80, (1, 2, 4)
NB = C // 16
ON_SCALAR = 3
INNER_AT = 11
CUTS = (0, 28, 62, K)
FLAG_CUT = 14
OUT_CUT = 12
DROP, LIFT, DROP4 = 2048.0, 32768.0, 512.0
BIG, HUGE = 2.0 ** 40, 2.0 ** 90
TILE0 = (0, 64, 128, 192, 128)
QUANT0 = (0, 64, 128, 192, 192)

SCRATCH = {}


def _buf(name, n, kind, where="sbuf"):
    SCRATCH[name] = (where, [128, n], kind)


def _mx(name, n):
    _buf("q" + name, n, MX)
    _buf("s" + name, n, U8)


for _n, _w, _k in (
        ("xt", 4 * C, BF), ("xs", 4 * C, BF), ("ut", 512, BF), ("vt", 512, BF), ("ones", 520, BF), ("el", 520, BF),
        ("ob1", 512, BF), ("ob2", 512, BF), ("t16", C, BF), ("t4", C, BF), ("mask", C, BF), ("nmask", C, BF),
        ("c16", C, BF), ("m4", C, BF), ("c4", C, BF), ("rst", 576, BF), ("nil", 576, BF), ("sd", C, BF), ("rc0", NB, F32), ("rc", NB, F32),
        ("x4", K, F32), ("xu", K, U16), ("la", 8, I32), ("lb", 32, I32), ("lj", 20, I32), ("lu", 8, U16), ("lv", 32, U16),
        ("pp", 1, I32), ("pi", 4, I32), ("pf", 8, F32),
        ("mkd", C, F32), ("bb", C, F32), ("hide", C, BF), ("fresh", C, BF), ("cor", C, BF), ("sg", 4 * C, BF), ("junk", 3072, BF),
        ("r0", NB, F32), ("ext", C, F32), ("t1", NB, F32), ("t2", NB, F32), ("rk", NB, F32), ("rku", NB, U16),
        ("rki", NB, I32), ("cei", NB, I32), ("ceu", NB, U16), ("t3", NB, F32), ("base", NB, F32),
        ("ob", C, BF), ("ex4", C, "float16"), ("ou", K, U16), ("tn", 4 * C, BF), ("am", 5 * C, BF), ("amp", 5 * C, BF),
        ("run", 4 * C, BF), ("mt", 512, BF), ("zt", 512, BF), ("dev", 8 * C, F32), ("vb", K, F32), ("flag", K, BF),
        ("fg", C, BF), ("fx", C, BF), ("ff", NB, F32), ("f0", NB, U16), ("f1", NB, U16), ("pl", C, BF), ("pg", 4 * C, BF),
        ("ys", C, F32)):
    _buf(_n, _w, _k)
for _c in range(5):
    _buf("ct%d" % _c, 4 * (C - TILE0[_c]), BF)
    _mx("c%d" % _c, C)
for _t in range(4):
    _mx("x%d" % _t, C)
for _t in range(3):
    _mx("m%d" % _t, 128 + K)
    _mx("z%d" % _t, 128 + K)
for _n, _w in (("u", 128), ("uo", 128), ("up0", 256), ("up1", 256), ("v", 128), ("w", 512), ("e", 512), ("o", 128)):
    _mx(_n, _w)
for _b in range(8):
    _buf("ps%d" % _b, 512, F32, "psum")

SEMAPHORES = ["ve", "ac", "pe", "po", "ldx", "ldu", "ldw", "ldv", "out", "left", "sent"]
SEMAPHORES += ["%s%d" % (_s, _t) for _s in ("am", "az", "sw") for _t in range(3)]


def _meet(a, b):
    if a[0] != b[0] or a[1] >= b[2] or b[1] >= a[2]:
        return False
    return not (a[3] == b[3] and (a[1] - b[1]) % a[3])


def _emit(g, T, ops):
    queue = {"ve": g.vector, "ac": g.scalar, "pe": g.tensor, "po": g, "sy": g.sync}
    total = {}
    for i, op in enumerate(ops):
        op["at"] = i
        total[op["sem"]] = total.get(op["sem"], 0) + op["inc"]
        op["count"] = total[op["sem"]]
    known = {e: {} for e in queue}
    group = {}
    for i, op in enumerate(ops):
        e = op["eng"]
        if e is None:
            op["seen"] = {}
            continue
        need = {}
        for old in ops[:i]:
            hit = any(_meet(a, b) for a in op["w"] for b in old["w"] + old["r"]) or any(_meet(a, b) for a in op["r"] for b in old["w"])
            if not hit and old["eng"] != e:
                hit = any(a[0][:2] == "ps" and a[0] == b[0] for a in op["r"] for b in old["r"])
            if hit and op["acc"] and old["acc"] == op["acc"]:
                hit = False
            if hit or old["tag"] in op["after"]:
                s = old["sem"]
                n = old["count"] if s in ("ve", "ac", "pe", "po", "sent") else total[s]
                if n > need.get(s, (0, None))[0]:
                    need[s] = (n, old)
        mine = known[e]
        order = sorted(need, key=lambda s: -need[s][1]["at"])
        for s in order:
            n, old = need[s]
            if mine.get(s, 0) >= n:
                continue
            queue[e].wait_ge(T.sem[s], n)
            mine[s] = n
            for k, val in (old["seen"] if s in ("ve", "ac", "pe", "po", "sent") else group.get(s, {})).items():
                mine[k] = max(mine.get(k, 0), val)
        op["seen"] = dict(mine)
        if op["sem"] not in ("ve", "ac", "pe", "po", "sent"):
            both = group.setdefault(op["sem"], {})
            for k, val in mine.items():
                both[k] = max(both.get(k, 0), val)
        done = op["fn"](queue[e])
        if done is not None:
            done.then_inc(T.sem[op["sem"]], op["inc"])
    for s in total:
        g.wait_ge(T.sem[s], total[s])


def rank_program(g, core, T, topo):
    rank = T.rank_of(core)
    if rank is None:
        return
    n_ranks = len(T.cores)
    ops = []

    def v(name, a=0, b=None, step=1):
        if b is None:
            b = SCRATCH[name][1][1]
        ap = T[name][:, a:b] if step == 1 else T[name][:, a:b:step]
        if name[:2] == "ps":
            return (ap, (name, 0, 512, 1))
        return (ap, (name, a, b, step))

    def ind(win, off):
        return (win[0].indirect(off[0]), win[1], off[1])

    def put(eng, fn, w, r, sem=None, inc=1, acc=None, tag=None, after=()):
        ops.append({"eng": eng, "fn": fn, "w": [k for x in w for k in x[1:]], "r": [k for x in r for k in x[1:]],
                    "sem": sem or eng, "inc": inc, "acc": acc, "tag": tag, "after": after})

    def arg(s):
        return s[0] if isinstance(s, tuple) else s

    def aps(*xs):
        return [x for x in xs if isinstance(x, tuple)]

    def copy(o, i):
        put("ve", lambda q: q.tensor_copy(o[0], i[0]), [o], [i])

    def tt(o, a, b, op):
        put("ve", lambda q: q.tensor_tensor(o[0], a[0], b[0], op), [o], [a, b])

    def ts(o, a, s1, op0, s2=None, op1=None):
        if op1 is None:
            put("ve", lambda q: q.tensor_scalar(o[0], a[0], arg(s1), None, op0), [o], aps(a, s1))
        else:
            put("ve", lambda q: q.tensor_scalar(o[0], a[0], arg(s1), arg(s2), op0, op1), [o], aps(a, s1, s2))

    def scan(o, d0, d1, init, op0, op1):
        put("ve", lambda q: q.tensor_tensor_scan(o[0], d0[0], d1[0], init, op0, op1), [o], [d0, d1])

    def fill(o, c):
        put("ve", lambda q: q.memset(o[0], c), [o], [])

    def act(o, i, f, bias=None, scale=None, acc=None):
        kw = {}
        if bias is not None:
            kw["bias"] = arg(bias)
        if scale is not None:
            kw["scale"] = arg(scale)
        if acc is not None:
            kw["accum_out"] = acc[0]
        put("ac", lambda q: q.activation(o[0], i[0], f, **kw), aps(o, acc), aps(i, bias, scale))

    def iota(o, pattern, base=0, mult=0):
        if SCRATCH[o[1][0]][2] == I32:
            put("po", lambda q: q.iota(o[0], pattern, base, mult), [o], [])
        else:
            put("po", lambda q: q.iota(o[0], pattern, base, mult, allow_small_or_imprecise_dtypes=True), [o], [])

    def select(o, i, pattern, op, base, mult, other=0.0):
        put("po", lambda q: q.affine_select(o[0], i[0], pattern, op, other, base, mult), [o], [i])

    def quant(name, a, b, i):
        qo, so = v("q" + name, a, b), v("s" + name, a, b)
        put("ve", lambda q: q.quantize_mx(qo[0], so[0], i[0]), [qo, so], [i])

    def mm(bank, lhs, rhs, start=True, stop=True, acc=None):
        o = v("ps%d" % bank, 0, rhs[2] - rhs[1])
        x = [v(p + s[0], s[1], s[2]) for s in (lhs, rhs) for p in "qs"]
        put("pe", lambda q: q.matmul_mx(o[0], x[0][0], x[1][0], x[2][0], x[3][0], start, stop), [o], x, acc=acc)

    def dma(eng, sem, o, i, w, r, after=(), tag=None):
        put(eng, lambda q: q.dma_start(o, i), w, r, sem=sem, inc=16, after=after, tag=tag)

    def pick_codes(name, off):
        o, win = v("q" + name), v("qu")
        put("ve", lambda q: q.tensor_copy(o[0].bitcast(dt.uint32), win[0].bitcast(dt.uint32).indirect(off[0])), [o], [win, off])

    def pick_scales(name, off):
        act(v("s" + name), ind(v("su"), off), ACT.Copy)

    def send(name, dst, sem, tag):
        rid, pid, _ = topo.addr(dst)
        far = [topo.engines(a, b) for a in T.cores for b in T.cores if a != b]
        use = [e for e in topo.engines(core, dst) if all(e in f for f in far)]
        mask = sum(1 << e for e in use)
        for p in "qs":
            src, land = v(p + name, 0, K), v(p + name, 128, 128 + K)

            def call(q, p=p, src=src, land=land):
                a, b = (land[0].bitcast(dt.uint8), src[0].bitcast(dt.uint8)) if p == "q" else (land[0], src[0])
                q.remote_dma(a, b, T.sem[sem], T.sem["left"], pid, rid, mask)
            put("po", call, [], [src], sem="left", inc=len(use))
        if tag:
            put("po", lambda q: (q.sem_inc(T.sem["sent"], 1), None)[1], [], [], sem="sent", tag=tag)
        put(None, None, [v("q" + name, 128, 128 + K), v("s" + name, 128, 128 + K)], [], sem=sem, inc=2 * len(use))

    col = lambda name, c: v(name, c, c + 1)
    ends = lambda name: v(name, 15, C, 16)

    dma("ac", "ldu", T.ut[:], T.u[:], [v("ut")], [])
    dma("sy", "ldx", T.xt[:], T.x[:], [v("xt")], [], tag="x")
    dma("sy", "ldw", T.qw[:].bitcast(dt.uint8), T.wc[:], [v("qw")], [], after=("x",))
    dma("sy", "ldw", T.sw[:], T.ws[:], [v("sw")], [])
    dma("sy", "ldv", T.vt[:], T.v[:], [v("vt")], [])

    fill(v("ones"), 1.0)
    iota(v("la"), [[16, 8]])
    iota(v("pp"), [[0, 1]], 0, 1)
    iota(v("t16"), [[0, NB], [1, 16]])
    iota(v("rc0"), [[16, NB]])
    select(v("el", 0, 516), v("ones", 0, 516), [[1, 516]], ALU.is_equal, -3, -4)
    select(v("ob1"), v("ones", 0, 512), [[-16, 8], [0, 64]], ALU.is_ge, 0, 1)
    select(v("ob2"), v("ob1"), [[16, 8], [0, 64]], ALU.is_ge, 15, -1)
    iota(v("sd"), [[1, C]], -C // 2)
    iota(v("nil"), [[0, 576]])
    iota(v("lb", 0, 16), [[16, 2], [32, 4], [0, 2]])
    iota(v("lj"), [[-112, 2], [32, 5], [0, 2]], 112)
    iota(v("x4"), [[4, K]])
    fill(v("ct4"), 0.0)
    fill(col("r0", NB - 1), 0.0)
    for c in range(4):
        act(v("t4", c, C, 4), v("ones", 0, K), ACT.Copy, scale=float(c))
    act(v("ct0", 0, 192), v("ones", 0, 192), ACT.Copy, scale=0.0)
    act(v("fresh"), v("t16"), ACT.Identity, bias=HUGE / 2, scale=-HUGE)
    copy(v("lu"), v("la"))
    ts(col("pi", 0), v("pp"), 15, ALU.bitwise_and)
    ts(col("pi", 1), v("pp"), 3, ALU.bitwise_and)
    ts(col("pi", 2), v("pp"), 2, ALU.logical_shift_right, 3, ALU.bitwise_and)
    quant("c1", 0, 128, v("ct4", 0, 512))
    copy(v("pf", 0, 3), v("pi", 0, 3))
    quant("c2", 0, 128, v("ct4", 0, 512))
    ts(v("mask"), v("t16"), col("pf", 0), ALU.is_equal)
    act(v("hide"), v("mask"), ACT.Identity, bias=HUGE / 2, scale=-HUGE)
    ts(col("pf", 3), col("pf", 0), -DROP, ALU.mult, 15 * DROP, ALU.add)
    ts(col("pf", 4), col("pf", 1), -DROP4, ALU.mult, 3 * DROP4 + C // 2, ALU.add)
    quant("c3", 0, 192, v("ct4"))
    ts(col("pf", 5), col("pf", 2), float(C), ALU.mult, col("pf", 4), ALU.add)
    tt(col("pf", 6), col("pf", 0), col("pf", 3), ALU.subtract)
    quant("u", 0, 128, v("ut"))
    quant("c4", 0, 192, v("ct4"))
    pick_codes("uo", v("lu"))
    pick_scales("uo", v("lu"))
    for c in range(1, 4):
        act(v("ct%d" % c, 0, 192), v("ones", 0, 192), ACT.Copy, scale=0.0)
    act(v("nmask"), v("mask"), ACT.Identity, bias=1.0, scale=-1.0)
    act(v("c16"), v("mask"), ACT.Identity, bias=-DROP, scale=LIFT + DROP)
    select(v("rst"), v("nil"), [[0, 144], [1, 4]], ALU.not_equal, 0, 0, -BIG)
    for name in ("mt", "zt"):
        iota(v(name, 4 * K, 512), [[0, 192]])
    ts(v("m4"), v("t4"), col("pf", 1), ALU.is_equal)
    ts(v("rc"), v("rc0"), col("pf", 6), ALU.add)
    for b in range(2):
        quant("e", 128 * b, 128 * b + 128, v("el", 3 - b, 515 - b))

    for t in range(3):
        xn = "x%d" % t
        helper = T.cores[(rank + STEP[t]) % n_ranks]
        client = T.cores[(rank - STEP[t]) % n_ranks]
        quant(xn, 0, C, v("xt" if t == 0 else "xs"))
        mm(0, ("uo", 0, 128), (xn, 0, C))
        mm(1, ("uo", 0, 128), (xn, 0, C))
        if t == 0:
            for b in range(2, 4):
                quant("e", 128 * b, 128 * b + 128, v("el", 3 - b, 515 - b))
        for b in range(4):
            mm(4 + b, ("e", 128 * b, 128 * b + 128), (xn, 0, C))
        for a, b in ((0, 16 * ON_SCALAR), (16 * ON_SCALAR, C)):
            tt(v("mkd", a, b), v("ps0", a, b), v("hide", a, b), ALU.max)
            scan(v("bb", a, b), v("fresh", a, b), v("mkd", a, b), 0.0, ALU.max, ALU.min)

        def slot(m):
            c = (m + 1) // 4
            return v("ct%d" % c, 4 * (16 * m + 16 - TILE0[c]) + (m + 1) % 4, 4 * (C - TILE0[c]), 4)

        for m in range(ON_SCALAR):
            act(v("sg", m * C + 16 * m + 16, (m + 1) * C), v("ps1", 16 * m + 16, C), ACT.Sign, bias=col("bb", 16 * m + 15), scale=-1.0)
        for m in range(ON_SCALAR):
            act(slot(m), v("sg", m * C + 16 * m + 16, (m + 1) * C), ACT.Relu, scale=-1.0, acc=col("r0", m))
        tiles = []

        def count(c):
            quant("c%d" % c, QUANT0[c], C, v("ct%d" % c, 4 * (QUANT0[c] - TILE0[c])))
            mm(2, ("o", 0, 128), ("c%d" % c, 0, C), start=not tiles, stop=len(tiles) == 4, acc="cs%d" % t)
            tiles.append(c)

        at = 0
        for m in range(ON_SCALAR, NB - 1):
            ts(slot(m), v("ps0", 16 * m + 16, C), col("bb", 16 * m + 15), ALU.is_gt)
            w = C - 16 * m - 16
            act(v("junk", at, at + w), slot(m), ACT.Identity, acc=col("r0", m))
            at += w
            if m == 7 and t == 0:
                quant("o", 0, 128, v("ob2"))
            if m in (7, 11, 15):
                count(m // 4)
            if m == INNER_AT:
                tt(slot(-1), v("ps0", 0, C), v("bb"), ALU.is_gt)
            if m == INNER_AT + 1:
                count(0)
        count(4)
        for b in range(4):
            if t == 0 and b == 2:
                act(v("c4"), v("m4"), ACT.Identity, bias=-DROP4, scale=5 * DROP4)
            act(v("tn", C * b, C * b + C), v("ps%d" % (4 + b), 0, C), ACT.Copy)
        scan(v("cor"), v("nmask"), slot(-1), 0.0, ALU.mult, ALU.add)
        tt(v("t1"), v("rc"), ends("cor"), ALU.add)
        tt(v("t2"), v("t1"), v("r0"), ALU.add)
        scan(v("ext"), v("c16"), v("ps2", 0, C), 0.0, ALU.add, ALU.min)
        tt(v("rk"), v("t2"), ends("ext"), ALU.subtract)
        copy(v("rku"), v("rk"))
        put("ve", lambda q: q.tensor_copy(T.ob[:].indirect(T.rku[:]), T.sd[:]), [v("ob")], [v("rku"), v("sd")])
        cuts = CUTS
        runs = ((cuts[1], K), (0, cuts[1]))
        for a, b in runs:
            scan(v("ex4", 4 * a, 4 * b), v("c4", 4 * a, 4 * b), v("ob", 4 * a, 4 * b), 0.0, ALU.add, ALU.min)
        for a, b in runs:
            ts(v("ou", a, b), v("ex4", 4 * a + 3, 4 * b, 4), col("pf", 5), ALU.add)
        copy(v("am", 0, 16 * cuts[1]), ind(v("tn"), v("ou", 0, cuts[1])))
        for j in (1, 2):
            act(v("am", 16 * cuts[j], 16 * cuts[j + 1]), ind(v("tn"), v("ou", cuts[j], cuts[j + 1])), ACT.Copy)
        for j in range(3):
            a, b = 16 * cuts[j], 16 * cuts[j + 1]
            scan(v("run", a, b), v("rst", 0, b - a), v("am", a, b), 0.0, ALU.add, ALU.max)
            if j == 2:
                copy(v("mt", 0, a // 4), v("run", 3, a, 4))
                copy(v("mt", a // 4, C), v("run", a + 3, b, 4))
        act(v("am", 4 * C, 5 * C), v("run", 3, 4 * C, 4), ACT.Copy, scale=-1.0)
        quant("m%d" % t, 0, 128, v("mt"))
        send("m%d" % t, helper, "am%d" % t, "m%d" % t)
        for k in range(8):
            e = (k ^ 1) if t % 2 == 0 else (((k + 1) ^ 1) - 1) % 8
            dma("sy", "sw%d" % t, T.amp[16 * k:16 * k + 16, :], T.am[16 * e:16 * e + 16, :],
                [(None, ("amp", k, 5 * C, 8))], [v("am")], after=("m%d" % t,))
        if t == 0:
            ts(v("xu"), v("x4"), col("pf", 2), ALU.add)
        tt(v("dev", 0, 4 * C), ind(v("am", 4 * C, 5 * C), v("xu")), v("am", 0, 4 * C), ALU.add)
        for b in range(4):
            mm(4 + b, ("w", 128 * b, 128 * b + 128), ("m%d" % t, K, 128 + K))
        for b in range(4):
            o, i = v("zt", b, 4 * K, 4), v("ps%d" % (4 + b), 128 - K, 128)
            if b % 2:
                ts(o, i, 0.015625, ALU.mult)
            else:
                act(o, i, ACT.Copy, scale=0.015625)
        quant("z%d" % t, 0, 128, v("zt"))
        send("z%d" % t, client, "az%d" % t, None)
        if t == 0:
            ts(v("lb", 16, 24), v("lj", 1, 9), 127, ALU.bitwise_and)
            ts(v("lb", 24, 32), v("lj", 11, 19), 127, ALU.bitwise_and)
            copy(v("lv"), v("lb"))
        if t < 2:
            pick_codes("up%d" % t, v("lv", 16 * t, 16 * t + 16))
            pick_scales("up%d" % t, v("lv", 16 * t, 16 * t + 16))
        else:
            quant("v", 0, 128, v("vt"))
        copy(v("rki"), v("rk"))
        ts(v("cei"), v("rki"), 2, ALU.logical_shift_right)
        copy(v("ceu"), v("cei"))
        ts(v("t3"), v("cei"), 12.0, ALU.mult, col("pf", 3), ALU.add)
        tt(v("base"), v("t3"), v("rk"), ALU.add)
        tt(v("dev", 4 * C, 8 * C), ind(v("amp", 4 * C, 5 * C), v("xu")), v("amp", 0, 4 * C), ALU.add)
        up, zin = "up%d" % (t % 2), ("z%d" % t, K, 128 + K)
        mm(1, (up, 128, 256), zin)
        mm(4, ("e", 0, 128), zin)
        mm(0, (up, 0, 128), zin)
        for b in range(1, 4):
            mm(4 + b, ("e", 128 * b, 128 * b + 128), zin)
        act(v("vb"), v("ps1", 128 - K, 128), ACT.Copy)
        copy(v("pl", 0, K), v("ps4", 128 - K, 128))
        tt(v("flag"), v("ps0", 128 - K, 128), v("vb"), ALU.is_lt)
        act(v("pl", K, 2 * K), v("ps5", 128 - K, 128), ACT.Copy)
        act(v("fg", 16 * FLAG_CUT, C), ind(v("flag"), v("ceu", FLAG_CUT, NB)), ACT.Copy, scale=4.0 * C)
        ts(v("fg", 0, 16 * FLAG_CUT), ind(v("flag"), v("ceu", 0, FLAG_CUT)), 4.0 * C, ALU.mult)
        act(v("pl", 2 * K, 3 * K), v("ps6", 128 - K, 128), ACT.Copy)
        scan(v("fx"), v("c16"), v("fg"), 0.0, ALU.add, ALU.min)
        tt(v("ff"), ends("fx"), v("base"), ALU.add)
        copy(v("f0"), v("ff"))
        ts(v("f1"), v("ff"), 4.0, ALU.add)
        for h, (lo, hi) in enumerate(((0, NB),) if t < 2 else ((0, OUT_CUT), (OUT_CUT, NB))):
            for b in range(4):
                if b == 2 and h == 0:
                    act(v("pl", 3 * K, 4 * K), v("ps7", 128 - K, 128), ACT.Copy)
                pg = v("pg", C * b + 16 * lo, C * b + 16 * hi)
                act(pg, ind(v("pl", K * b, K * b + K), v("ceu", lo, hi)), ACT.Copy)
                tt(v("xs", 64 * lo + b, 64 * hi, 4), ind(v("dev", 8 * (b // 2)), v("f%d" % (b % 2), lo, hi)), pg, ALU.add)
            if t < 2:
                continue
            a, b = 16 * lo, 16 * hi
            quant("x3", a, b, v("xs", 4 * a, 4 * b))
            mm(h, ("v", 0, 128), ("x3", a, b))
            if h == 1:
                act(v("ys", 0, a), v("ps0", 0, a), ACT.Copy)
                dma("sy", "out", T.y[:, 0:a], T.ys[:, 0:a], [], [v("ys", 0, a)])
            dma("sy", "out", T.oc[:, 4 * a:4 * b], T.qx3[:, a:b].bitcast(dt.uint8), [], [v("qx3", a, b)])
            if h == 0:
                continue
            for k in range(4):
                dma("ac", "out", T.osc[4 * k:4 * k + 4, :], T.sx3[32 * k:32 * k + 4, :], [], [v("sx3")])
            copy(v("ys", a, b), v("ps1", 0, b - a))
            dma("sy", "out", T.y[:, a:b], T.ys[:, a:b], [], [v("ys", a, b)])
    _emit(g, T, ops)
